import numpy as np
import ml_dtypes


def mxq(x, axis, fmt="e4m3"):
    dtype, down = {"e4m3": (ml_dtypes.float8_e4m3fn, 7), "e5m2": (ml_dtypes.float8_e5m2, 14)}[fmt]
    v = np.moveaxis(np.asarray(x, np.float32).astype(ml_dtypes.bfloat16).astype(np.float64), axis, -1)
    blocks = v.reshape(v.shape[:-1] + (-1, 32))
    amax = np.abs(blocks).max(-1, keepdims=True)
    byte = np.maximum(np.where(amax > 0, np.frexp(amax)[1] - 1 + 127, 0) - down, 1)
    scale = np.exp2(byte - 127.0)
    codes = (blocks / scale).astype(np.float32).astype(dtype).astype(np.float64)
    return np.moveaxis((codes * scale).reshape(v.shape), -1, axis)


WIDE = False


def mx_kscale(k):
    if not WIDE:
        return np.ones(k)
    levels = np.array([10, -10, 5, -5, 0])
    if k % 512:
        return np.exp2(np.random.permutation(np.resize(levels, k // 32))).repeat(32)
    a = np.empty((k // 512, 16))
    for p in range(k // 512):
        a[p, :8] = np.random.permutation(np.resize(levels, 8))
        for g in range(8):
            far = levels[np.abs(levels - a[p, g]) >= 10]
            a[p, g + 8] = far[np.random.randint(len(far))]
    return np.exp2(a.ravel()).repeat(32)


def f64(x):
    return np.asarray(x).astype(np.float64)


def striped(idx):
    return np.tile(np.asarray(idx).reshape(-1, 16).T, (8, 1)).astype(np.uint16)


def unstriped(offs):
    return offs[:16].T.reshape(-1).astype(np.int64)


E2M1 = np.array([0.0, 0.5, 1.0, 1.5, 2.0, 3.0, 4.0, 6.0, -0.0, -0.5, -1.0, -1.5, -2.0, -3.0, -4.0, -6.0])


def pack_weight(w, fmt):
    k, n = w.shape
    w = f64(np.asarray(w, np.float32).astype(ml_dtypes.bfloat16)).reshape(k // 32, 32, n)
    amax = np.abs(w).max(1)
    if fmt == "e4m3":
        byte = np.frexp(amax)[1] - 1 + 127 - 7
    else:
        mant, ex = np.frexp(amax / 6.0)
        byte = np.where(mant > 0.5, ex, ex - 1) + 127
    byte = np.clip(np.where(amax > 0, byte, 1), 1, 254)
    scaled = (w * np.exp2(127.0 - byte)[:, None, :]).reshape(k, n).astype(np.float32)
    by_word = np.ascontiguousarray(scaled.reshape(k // 512, 128, 4, n).transpose(0, 1, 3, 2))
    if fmt == "e4m3":
        words = by_word.astype(ml_dtypes.float8_e4m3fn).view(np.uint8)
    else:
        c = by_word.astype(ml_dtypes.float4_e2m1fn).view(np.uint8) & 0xF
        words = (c[..., 0::2] | (c[..., 1::2] << 4)).reshape(k // 512, 128, 2 * n)
    return np.ascontiguousarray(words), np.ascontiguousarray(byte.astype(np.uint8).reshape(k // 512, 16, n))


def unpack_weight(words, scales, fmt):
    g, _, n = scales.shape
    words = np.ascontiguousarray(words).reshape(g, 128, n, -1)
    if fmt == "e4m3":
        vals = words.view(ml_dtypes.float8_e4m3fn).astype(np.float64)
    else:
        nib = np.empty((g, 128, n, 4), np.uint8)
        nib[..., 0::2] = words & 0xF
        nib[..., 1::2] = words >> 4
        vals = E2M1[nib]
    vals = vals * np.repeat(np.exp2(scales.astype(np.float64) - 127.0), 8, axis=1)[..., None]
    return vals.transpose(0, 1, 3, 2).reshape(g * 512, n)


def bf(x):
    return np.asarray(x, np.float32).astype(ml_dtypes.bfloat16)


def planes(Y):
    r, m = Y.shape
    b = f64(bf(Y)).reshape(r // 32, 32, m)
    amax = np.abs(b).max(1)
    byte = np.clip(np.where(amax > 0, np.frexp(amax)[1] - 1 + 127 - 7, 1), 1, 254)
    codes = (b * np.exp2(127.0 - byte)[:, None, :]).reshape(r, m).astype(np.float32).astype(ml_dtypes.float8_e4m3fn).view(np.uint8)
    words = codes.reshape(r // 512, 128, 4, m).transpose(0, 1, 3, 2)
    return np.ascontiguousarray(words), np.ascontiguousarray(byte.astype(np.uint8).reshape(r // 512, 16, m))


D, T, I, J, U, Z, E, M = 512, 2048, 512, 512, 1024, 1024, 512, 1024


def setup_inputs():
    n = np.random.standard_normal
    idx = np.random.permutation(T)[:I]
    idx2 = np.random.permutation(U)[:J]
    idx3 = np.random.permutation(Z)[:J]
    idx4 = np.random.permutation(M)[:J]
    fd = mx_kscale(D)
    fi = mx_kscale(I)
    ti = np.ones(T)
    ti[idx] = fi
    keysp = pack_weight(n((D, T)) / fd[:, None], "e2m1")
    return {
        "keys_words": keysp[0],
        "keys_scales": keysp[1],
        "notes": (n((D, U)) * 1.0 / np.sqrt(D) * fd[:, None]).astype(np.float32),
        "users2": (n((D, Z)) * 1.0 / np.sqrt(D) * fd[:, None]).astype(np.float32),
        "rowf": (np.random.uniform(0.02, 0.08, (I, 1)) * fi[:, None]).astype(np.float32),
        "vals": (n((E, T)) / ti).astype(np.float32),
        "old": (1.0 * n((E, M))).astype(np.float32),
        "offs": striped(idx),
        "offs2": striped(idx2),
        "offs3": striped(idx3),
        "offs4": striped(idx4),
    }


def reference(keys_words, keys_scales, notes, users2, rowf, vals, old, offs, offs2, offs3, offs4):
    idx = unstriped(offs)
    idx2 = unstriped(offs2)
    idx3 = unstriped(offs3)
    idx4 = unstriped(offs4)
    keysu = unpack_weight(keys_words, keys_scales, "e2m1")
    keysidxg = keysu[:, idx]
    notesidx2q = mxq(f64(notes)[:, idx2], 0, "e4m3")
    g1 = keysidxg.T @ notesidx2q
    users2idx3q = mxq(f64(users2)[:, idx3], 0, "e4m3")
    g2 = keysidxg.T @ users2idx3q
    g0 = np.maximum(g1, g2)
    gr1 = g0 * f64(rowf)
    vt1 = f64(vals)[:, idx].T
    vt1q = mxq(vt1, 0, "e4m3")
    gr1q = mxq(gr1, 0, "e4m3")
    o = vt1q.T @ gr1q
    of = np.zeros((E, M))
    of[:, idx4] = o
    y = f64(old) + of
    words, scales = planes(y)
    return y, words, scales

@@ -1,0 +1,276 @@
+from contextlib import ExitStack
+
+import concourse.mybir as mybir
+from concourse.masks import make_identity
+
+D, T, I, J, U, Z, E, M = 512, 2048, 512, 512, 1024, 1024, 512, 1024
+FLOPS = 2 * D * I * J * 2 + 2 * I * E * J
+
+F32 = mybir.dt.float32
+BF16 = mybir.dt.bfloat16
+I32 = mybir.dt.int32
+U32 = mybir.dt.uint32
+U16 = mybir.dt.uint16
+U8 = mybir.dt.uint8
+FP8X4 = mybir.dt.float8_e4m3fn_x4
+FP4X4 = mybir.dt.float4_e2m1fn_x4
+COPY = mybir.ActivationFunctionType.Copy
+ALU = mybir.AluOpType
+
+P = 128
+PACK = 4
+JB = 128
+JH = 256
+MH = 512
+
+
+def tile_attend_tab_larger_put_pl_kernel(
+    tc, keys_words, keys_scales, notes, users2, rowf, vals, old, offs, offs2, offs3, offs4, out_0, out_1, out_2
+):
+    nc = tc.nc
+    with ExitStack() as ctx:
+        sb = ctx.enter_context(tc.tile_pool(name="sb", bufs=1))
+        ps = ctx.enter_context(tc.psum_pool(name="ps", bufs=1))
+
+        def tiles(name, n, shape, dtype):
+            return [sb.tile(shape, dtype, name="%s%d" % (name, k), align_bytes=64) for k in range(n)]
+
+        def one(name, shape, dtype):
+            return sb.tile(shape, dtype, name=name, align_bytes=64)
+
+        l_tok = one("l_tok", [P, I // 16], U16)
+        l_note = one("l_note", [P, J // 16], U16)
+        l_user = one("l_user", [P, J // 16], U16)
+        l_put = one("l_put", [P, J // 16], U16)
+        kw = one("kw", [P, T], U16)
+        ks = one("ks", [P, T], U8)
+        nt = tiles("nt", PACK, [P, U], F32)
+        ut = tiles("ut", PACK, [P, Z], F32)
+        vt = tiles("vt", PACK, [P, T], F32)
+        ot = tiles("ot", PACK, [P, M], F32)
+        of = tiles("of", PACK, [P, M], F32)
+        rf = one("rf", [P, PACK], F32)
+        ident = one("ident", [P, P], F32)
+
+        notes_v = notes.rearrange("(p t) u -> p t u", t=PACK)
+        users_v = users2.rearrange("(p t) u -> p t u", t=PACK)
+        vals_v = vals.rearrange("(p t) u -> p t u", t=PACK)
+        old_v = old.rearrange("(p t) u -> p t u", t=PACK)
+        out_v = out_0.rearrange("(p t) u -> p t u", t=PACK)
+
+        nc.vector.memset(ks[:].bitcast(I32), 0)
+        kst = one("kst", [4, 4, T // 4], I32)
+        nc.sync.dma_start(kst[:], keys_scales[0].bitcast(I32).rearrange("(q c) n -> c q n", c=4))
+        nc.sync.dma_start(l_note[:], offs2)
+        nc.sync.dma_start(nt[0][:], notes_v[:, 0, :])
+        nc.sync.dma_start(l_tok[:], offs)
+        nc.sync.dma_start(kw[:].bitcast(I32), keys_words[0].bitcast(I32))
+        for t in range(1, PACK):
+            nc.sync.dma_start(nt[t][:], notes_v[:, t, :])
+        nc.sync.dma_start(l_user[:], offs3)
+        for t in range(PACK):
+            nc.sync.dma_start(ut[t][:], users_v[:, t, :])
+        nc.sync.dma_start(rf[:], rowf.rearrange("(p r) one -> p (r one)", r=PACK))
+        nc.sync.dma_start(vt[0][:], vals_v[:, 0, :])
+        nc.sync.dma_start(l_put[:], offs4)
+        for t in range(1, PACK):
+            nc.sync.dma_start(vt[t][:], vals_v[:, t, :])
+        for t in range(PACK):
+            nc.sync.dma_start(ot[t][:], old_v[:, t, :])
+
+        make_identity(nc, ident[:])
+        for r in range(PACK):
+            nc.vector.memset(of[r][:], 0.0)
+
+        def gather(on_vector, out, window, offsets):
+            if on_vector:
+                nc.vector.tensor_copy(out, window.indirect(offsets))
+            else:
+                nc.scalar.activation(out, window.indirect(offsets), COPY)
+
+        def scatter(on_vector, window, offsets, values):
+            if on_vector:
+                nc.vector.tensor_copy(window.indirect(offsets), values)
+            else:
+                nc.scalar.activation(window.indirect(offsets), values, COPY)
+
+        def quantize(codes, scales, grouped):
+            nc.vector.quantize_mx(out=codes.bitcast(FP8X4), scales=scales, in_=grouped)
+
+        for q in range(4):
+            nc.vector.tensor_copy(ks[32 * q : 32 * q + 4, :].bitcast(I32), kst[:, q, :])
+        kwg = one("kwg", [P, I], U16)
+        nc.vector.tensor_copy(kwg[:], kw[:].indirect(l_tok[:]))
+        ksd = one("ksd", [P, I], U8)
+        nc.vector.tensor_copy(ksd[:].rearrange("p (r s) -> p s r", r=PACK), ks[:].indirect(l_tok[:]))
+        kwd = one("kwd", [P, I], U16)
+        nc.vector.tensor_copy(
+            kwd[:].rearrange("p (r s) -> p r s", r=PACK), kwg[:].rearrange("p (s r) -> p r s", r=PACK)
+        )
+        halves = [slice(h * JH, (h + 1) * JH) for h in range(2)]
+        lists = [slice(16 * h, 16 * h + 16) for h in range(2)]
+
+        def gather_planes(dst, planes, offsets, engines):
+            for t in range(PACK - 1):
+                gather(engines[t], dst[:, t, :], planes[t][:], offsets[:])
+            for h in range(2):
+                gather(h == 0, dst[:, PACK - 1, halves[h]], planes[PACK - 1][:], offsets[:, lists[h]])
+
+        def weave_quant(src, woven, codes, scales):
+            for h in range(2):
+                nc.vector.tensor_copy(woven[h][:], src[:, :, halves[h]].rearrange("p t j -> p j t"))
+                quantize(codes[h][:], scales[h][:], woven[h][:].rearrange("p j t -> p (j t)"))
+
+        ng = one("ng", [P, PACK, J], BF16)
+        gather_planes(ng, nt, l_note, [False, False, False])
+        ni = tiles("ni", 2, [P, JH, PACK], BF16)
+        nq = tiles("nq", 2, [P, JH], U32)
+        ns = tiles("ns", 2, [P, JH], U8)
+        weave_quant(ng, ni, nq, ns)
+
+        def scores(bank, codes, scales):
+            for r in range(PACK):
+                cols = slice(r * P, (r + 1) * P)
+                nc.tensor.matmul_mx(
+                    out=bank[:, r, :],
+                    lhsT=kwd[:, cols].bitcast(FP4X4),
+                    lhsT_scale=ksd[:, cols],
+                    rhs=codes.bitcast(FP8X4),
+                    rhs_scale=scales,
+                    start=True,
+                    stop=True,
+                )
+
+        g1 = tiles("g1", J // JB, [P, JB, PACK], F32)
+
+        def first_table(h):
+            for k in range(2):
+                cols = slice(k * JB, (k + 1) * JB)
+                bank = ps.tile([P, PACK, JB], F32, name="bank_g1", tag="acc", bufs=4)
+                scores(bank, nq[h][:, cols], ns[h][:, cols])
+                nc.scalar.copy(g1[2 * h + k][:], bank[:].rearrange("p r n -> p n r"))
+
+        first_table(0)
+        ug = one("ug", [P, PACK, J], BF16)
+        gather_planes(ug, ut, l_user, [False, False, True])
+        first_table(1)
+        ui = tiles("ui", 2, [P, JH, PACK], BF16)
+        uq = tiles("uq", 2, [P, JH], U32)
+        us = tiles("us", 2, [P, JH], U8)
+        weave_quant(ug, ui, uq, us)
+
+        g0 = tiles("g0", 2, [P, JH, PACK], F32)
+        gr = tiles("gr", 2, [P, JH, PACK], BF16)
+        gq = tiles("gq", 2, [P, JH], U32)
+        gs = tiles("gs", 2, [P, JH], U8)
+
+        def table(h):
+            for k in range(2):
+                cols = slice(k * JB, (k + 1) * JB)
+                bank = ps.tile([P, PACK, JB], F32, name="bank_g2", tag="g2", bufs=4)
+                scores(bank, uq[h][:, cols], us[h][:, cols])
+                nc.vector.tensor_tensor(
+                    g0[h][:, cols, :], bank[:].rearrange("p r n -> p n r"), g1[2 * h + k][:], ALU.max
+                )
+
+        def table_rows(h):
+            nc.vector.tensor_tensor(gr[h][:], g0[h][:], rf[:].unsqueeze(1).to_broadcast([P, JH, PACK]), ALU.mult)
+            quantize(gq[h][:], gs[h][:], gr[h][:].rearrange("p j t -> p (j t)"))
+
+        vg = tiles("vg", PACK, [P, I], BF16)
+        vi = tiles("vi", PACK, [P, P * PACK], BF16)
+        vq = tiles("vq", PACK, [P, P], U32)
+        vs = tiles("vs", PACK, [P, P], U8)
+        y = one("y", [P, PACK, M], F32)
+        yi = tiles("yi", M // MH, [P, MH, PACK], BF16)
+        yq = tiles("yq", M // MH, [P, MH], U32)
+        ys = one("ys", [P, M], U8)
+
+        def values_gather(r, on_vector):
+            gather(on_vector, vg[r][:], vt[r][:], l_tok[:])
+
+        def values(r, on_vector):
+            words = vg[r][:].bitcast(F32)
+            bank = ps.tile([P, 2, P], F32, name="bank_v", tag="g2", bufs=4)
+            for u in range(2):
+                nc.tensor.transpose(bank[:, u, :], words[:, u : I // 2 : 2], ident[:])
+            dst = vi[r][:].bitcast(F32).rearrange("p (m u) -> p m u", u=2)
+            src = bank[:].rearrange("p u m -> p m u")
+            if on_vector:
+                nc.vector.tensor_copy(dst, src)
+            else:
+                nc.scalar.copy(dst, src)
+            quantize(vq[r][:], vs[r][:], vi[r][:])
+
+        def product(r, h, on_vector):
+            bank = ps.tile([P, JH], F32, name="bank_o", tag="g2" if on_vector else "acc", bufs=4)
+            nc.tensor.matmul_mx(
+                out=bank[:],
+                lhsT=vq[r][:].bitcast(FP8X4),
+                lhsT_scale=vs[r][:],
+                rhs=gq[h][:].bitcast(FP8X4),
+                rhs_scale=gs[h][:],
+                start=True,
+                stop=True,
+            )
+            if on_vector:
+                piece = y[:, 0, halves[h]]
+            else:
+                piece = sb.tile([P, JH], F32, name="piece", bufs=2, align_bytes=64)[:]
+            if on_vector:
+                nc.vector.tensor_copy(piece, bank[:])
+            else:
+                nc.scalar.copy(piece, bank[:])
+            scatter(on_vector, of[r][:], l_put[:, 16 * h : 16 * h + 16], piece)
+
+        def add_old(r, cols, eng):
+            eng.tensor_tensor(y[:, r, cols], ot[r][:, cols], of[r][:, cols], ALU.add)
+            nc.sync.dma_start(out_v[:, r, cols], y[:, r, cols])
+
+        def round_pair(c, q, on_vector):
+            cols = slice(c * MH, (c + 1) * MH)
+            dst = yi[c][:, :, 2 * q : 2 * q + 2]
+            src = y[:, 2 * q : 2 * q + 2, cols].rearrange("p r m -> p m r")
+            if on_vector:
+                nc.vector.tensor_copy(dst, src)
+            else:
+                nc.scalar.copy(dst, src)
+
+        whole = slice(0, M)
+        table(0)
+        table_rows(0)
+        values_gather(0, False)
+        values(0, False)
+        product(0, 0, False)
+        table(1)
+        values_gather(1, False)
+        values(1, False)
+        product(1, 0, False)
+        values_gather(2, True)
+        table_rows(1)
+        values(2, True)
+        product(0, 1, False)
+        product(2, 0, True)
+        product(1, 1, False)
+        product(2, 1, True)
+        values_gather(3, False)
+        values(3, True)
+        product(3, 0, False)
+        product(3, 1, False)
+        add_old(0, whole, nc.vector)
+        add_old(1, whole, nc.vector)
+        add_old(2, whole, nc.vector)
+        round_pair(0, 0, True)
+        round_pair(1, 0, True)
+        for c in range(M // MH):
+            add_old(3, slice(c * MH, (c + 1) * MH), nc.vector)
+        round_pair(0, 1, False)
+        round_pair(1, 1, True)
+        words_out = out_1[0].rearrange("p m t -> p (m t)").bitcast(I32)
+        for c in (1, 0):
+            cols = slice(c * MH, (c + 1) * MH)
+            quantize(yq[c][:], ys[:, cols], yi[c][:].rearrange("p m t -> p (m t)"))
+            nc.sync.dma_start(words_out[:, cols], yq[c][:].bitcast(I32))
+        for q in range(4):
+            eng = nc.sync if q % 2 == 0 else nc.scalar
+            eng.dma_start(out_2[0, 4 * q : 4 * q + 4, :].bitcast(I32), ys[32 * q : 32 * q + 4, :].bitcast(I32))

@@ -32,11 +32,14 @@ def tile_attend_tab_larger_put_pl_kernel(
         sb = ctx.enter_context(tc.tile_pool(name="sb", bufs=1))
         ps = ctx.enter_context(tc.psum_pool(name="ps", bufs=1))
 
-        def tiles(name, n, shape, dtype):
-            return [sb.tile(shape, dtype, name="%s%d" % (name, k), align_bytes=64) for k in range(n)]
+        def one(name, shape, dtype, tag=None):
+            return sb.tile(shape, dtype, name=name, tag=tag or name, align_bytes=64)
 
-        def one(name, shape, dtype):
-            return sb.tile(shape, dtype, name=name, align_bytes=64)
+        def tiles(name, n, shape, dtype):
+            return [one("%s%d" % (name, k), shape, dtype) for k in range(n)]
+
+        def bank(name, shape, number):
+            return ps.tile(shape, F32, name=name, tag="bank%d" % number)
 
         l_tok = one("l_tok", [P, I // 16], U16)
         l_note = one("l_note", [P, J // 16], U16)
@@ -44,6 +47,7 @@ def tile_attend_tab_larger_put_pl_kernel(
         l_put = one("l_put", [P, J // 16], U16)
         kw = one("kw", [P, T], U16)
         ks = one("ks", [P, T], U8)
+        kst = one("kst", [4, 4, T // 4], I32)
         nt = tiles("nt", PACK, [P, U], F32)
         ut = tiles("ut", PACK, [P, Z], F32)
         vt = tiles("vt", PACK, [P, T], F32)
@@ -58,8 +62,6 @@ def tile_attend_tab_larger_put_pl_kernel(
         old_v = old.rearrange("(p t) u -> p t u", t=PACK)
         out_v = out_0.rearrange("(p t) u -> p t u", t=PACK)
 
-        nc.vector.memset(ks[:].bitcast(I32), 0)
-        kst = one("kst", [4, 4, T // 4], I32)
         nc.sync.dma_start(kst[:], keys_scales[0].bitcast(I32).rearrange("(q c) n -> c q n", c=4))
         nc.sync.dma_start(l_note[:], offs2)
         nc.sync.dma_start(nt[0][:], notes_v[:, 0, :])
@@ -79,8 +81,12 @@ def tile_attend_tab_larger_put_pl_kernel(
             nc.sync.dma_start(ot[t][:], old_v[:, t, :])
 
         make_identity(nc, ident[:])
+        nc.vector.memset(ks[:].bitcast(I32), 0)
         for r in range(PACK):
             nc.vector.memset(of[r][:], 0.0)
+
+        halves = [slice(h * JH, (h + 1) * JH) for h in range(2)]
+        lists = [slice(16 * h, 16 * h + 16) for h in range(2)]
 
         def gather(on_vector, out, window, offsets):
             if on_vector:
@@ -93,6 +99,12 @@ def tile_attend_tab_larger_put_pl_kernel(
                 nc.vector.tensor_copy(window.indirect(offsets), values)
             else:
                 nc.scalar.activation(window.indirect(offsets), values, COPY)
+
+        def copy(on_vector, out, in_):
+            if on_vector:
+                nc.vector.tensor_copy(out, in_)
+            else:
+                nc.scalar.copy(out, in_)
 
         def quantize(codes, scales, grouped):
             nc.vector.quantize_mx(out=codes.bitcast(FP8X4), scales=scales, in_=grouped)
@@ -107,8 +119,6 @@ def tile_attend_tab_larger_put_pl_kernel(
         nc.vector.tensor_copy(
             kwd[:].rearrange("p (r s) -> p r s", r=PACK), kwg[:].rearrange("p (s r) -> p r s", r=PACK)
         )
-        halves = [slice(h * JH, (h + 1) * JH) for h in range(2)]
-        lists = [slice(16 * h, 16 * h + 16) for h in range(2)]
 
         def gather_planes(dst, planes, offsets, engines):
             for t in range(PACK - 1):
@@ -118,21 +128,18 @@ def tile_attend_tab_larger_put_pl_kernel(
 
         def weave_quant(src, woven, codes, scales):
             for h in range(2):
-                nc.vector.tensor_copy(woven[h][:], src[:, :, halves[h]].rearrange("p t j -> p j t"))
+                nc.vector.tensor_copy(
+                    woven[h][:].rearrange("p (c i) t -> p c t i", i=4),
+                    src[:, :, halves[h]].rearrange("p t (c i) -> p c t i", i=4),
+                )
+            for h in range(2):
                 quantize(codes[h][:], scales[h][:], woven[h][:].rearrange("p j t -> p (j t)"))
 
-        ng = one("ng", [P, PACK, J], BF16)
-        gather_planes(ng, nt, l_note, [False, False, False])
-        ni = tiles("ni", 2, [P, JH, PACK], BF16)
-        nq = tiles("nq", 2, [P, JH], U32)
-        ns = tiles("ns", 2, [P, JH], U8)
-        weave_quant(ng, ni, nq, ns)
-
-        def scores(bank, codes, scales):
+        def scores(acc, codes, scales):
             for r in range(PACK):
                 cols = slice(r * P, (r + 1) * P)
                 nc.tensor.matmul_mx(
-                    out=bank[:, r, :],
+                    out=acc[:, r, :],
                     lhsT=kwd[:, cols].bitcast(FP4X4),
                     lhsT_scale=ksd[:, cols],
                     rhs=codes.bitcast(FP8X4),
@@ -141,87 +148,127 @@ def tile_attend_tab_larger_put_pl_kernel(
                     stop=True,
                 )
 
-        g1 = tiles("g1", J // JB, [P, JB, PACK], F32)
+        ng = one("ng", [P, PACK, J], BF16)
+        gather_planes(ng, nt, l_note, [False, False, False])
+        ni = tiles("ni", 2, [P, JH, PACK], BF16)
+        nq = tiles("nq", 2, [P, JH], U32)
+        ns = tiles("ns", 2, [P, JH], U8)
+        weave_quant(ng, ni, nq, ns)
 
-        def first_table(h):
-            for k in range(2):
-                cols = slice(k * JB, (k + 1) * JB)
-                bank = ps.tile([P, PACK, JB], F32, name="bank_g1", tag="acc", bufs=4)
-                scores(bank, nq[h][:, cols], ns[h][:, cols])
-                nc.scalar.copy(g1[2 * h + k][:], bank[:].rearrange("p r n -> p n r"))
-
-        first_table(0)
         ug = one("ug", [P, PACK, J], BF16)
         gather_planes(ug, ut, l_user, [False, False, True])
-        first_table(1)
+
+        g1 = []
+        for h in range(2):
+            g1.append(one("g1_%d" % h, [P, JH, PACK], F32, tag="ut%d" % (2 * h + 1)))
+            for k in range(2):
+                cols = slice(k * JB, (k + 1) * JB)
+                acc = bank("acc_g1", [P, PACK, JB], 2 * h + k)
+                scores(acc, nq[h][:, cols], ns[h][:, cols])
+                nc.scalar.copy(g1[h][:, cols, :], acc[:].rearrange("p r n -> p n r"))
+
         ui = tiles("ui", 2, [P, JH, PACK], BF16)
         uq = tiles("uq", 2, [P, JH], U32)
         us = tiles("us", 2, [P, JH], U8)
         weave_quant(ug, ui, uq, us)
 
         g0 = tiles("g0", 2, [P, JH, PACK], F32)
-        gr = tiles("gr", 2, [P, JH, PACK], BF16)
-        gq = tiles("gq", 2, [P, JH], U32)
+        gq = {}
         gs = tiles("gs", 2, [P, JH], U8)
 
-        def table(h):
-            for k in range(2):
-                cols = slice(k * JB, (k + 1) * JB)
-                bank = ps.tile([P, PACK, JB], F32, name="bank_g2", tag="g2", bufs=4)
-                scores(bank, uq[h][:, cols], us[h][:, cols])
-                nc.vector.tensor_tensor(
-                    g0[h][:, cols, :], bank[:].rearrange("p r n -> p n r"), g1[2 * h + k][:], ALU.max
-                )
+        def larger(h, k):
+            cols = slice(k * JB, (k + 1) * JB)
+            acc = bank("acc_g2", [P, PACK, JB], 4 + 2 * h + k)
+            scores(acc, uq[h][:, cols], us[h][:, cols])
+            nc.vector.tensor_tensor(g0[h][:, cols, :], acc[:].rearrange("p r n -> p n r"), g1[h][:, cols, :], ALU.max)
 
-        def table_rows(h):
+        gr = {}
+
+        def scale_rows(h, tag):
+            gr[h] = one("gr%d" % h, [P, JH, PACK], BF16, tag=tag)
             nc.vector.tensor_tensor(gr[h][:], g0[h][:], rf[:].unsqueeze(1).to_broadcast([P, JH, PACK]), ALU.mult)
+
+        def quant_table(h, tag):
+            gq[h] = one("gq%d" % h, [P, JH], U32, tag=tag)
             quantize(gq[h][:], gs[h][:], gr[h][:].rearrange("p j t -> p (j t)"))
 
         vg = tiles("vg", PACK, [P, I], BF16)
-        vi = tiles("vi", PACK, [P, P * PACK], BF16)
         vq = tiles("vq", PACK, [P, P], U32)
         vs = tiles("vs", PACK, [P, P], U8)
-        y = one("y", [P, PACK, M], F32)
+
+        woven_values = {}
+
+        def turn_values(r, on_vector, number, tag):
+            words = vg[r][:].bitcast(F32)
+            acc = bank("acc_v", [P, 2, P], number)
+            for u in range(2):
+                nc.tensor.transpose(acc[:, u, :], words[:, u : I // 2 : 2], ident[:])
+            vi = one("vi%d" % r, [P, P * PACK], BF16, tag=tag)
+            copy(on_vector, vi[:].bitcast(F32).rearrange("p (m u) -> p m u", u=2), acc[:].rearrange("p u m -> p m u"))
+            woven_values[r] = vi
+
+        def quant_values(r):
+            quantize(vq[r][:], vs[r][:], woven_values[r][:])
+
+        pieces = {}
+
+        def products(name, units, on_vector, number, tag):
+            acc = bank("acc_o", [P, J], number)
+            for k, (r, h) in enumerate(units):
+                nc.tensor.matmul_mx(
+                    out=acc[:, halves[k]],
+                    lhsT=vq[r][:].bitcast(FP8X4),
+                    lhsT_scale=vs[r][:],
+                    rhs=gq[h][:].bitcast(FP8X4),
+                    rhs_scale=gs[h][:],
+                    start=True,
+                    stop=True,
+                )
+            staged = one(name, [P, J], F32, tag=tag)
+            copy(on_vector, staged[:], acc[:])
+            for k, unit in enumerate(units):
+                pieces[unit] = staged[:, halves[k]]
+
+        def put(r, h, on_vector):
+            scatter(on_vector, of[r][:], l_put[:, lists[h]], pieces[r, h])
+
+        larger(0, 0)
+        larger(0, 1)
+        larger(1, 0)
+        scale_rows(0, None)
+        gather(False, vg[0][:], vt[0][:], l_tok[:])
+        gather(False, vg[1][:], vt[1][:], l_tok[:])
+        turn_values(0, False, 0, "vt1")
+        turn_values(1, False, 1, None)
+        quant_values(0)
+        quant_table(0, None)
+        quant_values(1)
+        larger(1, 1)
+        gather(False, vg[2][:], vt[2][:], l_tok[:])
+        products("first", ((0, 0), (1, 0)), False, 1, "vt2")
+        turn_values(2, True, 4, None)
+        scale_rows(1, "vi1")
+        gather(True, vg[3][:], vt[3][:], l_tok[:])
+        quant_table(1, "vt3")
+        quant_values(2)
+        put(0, 0, False)
+        put(1, 0, False)
+        products("second", ((0, 1), (1, 1)), False, 4, "vt2")
+        turn_values(3, True, 5, None)
+        quant_values(3)
+        products("own", ((2, 0), (2, 1)), True, 6, "late")
+        put(2, 0, True)
+        put(2, 1, True)
+        put(0, 1, False)
+        put(1, 1, False)
+        products("third", ((3, 0), (3, 1)), False, 0, None)
+        put(3, 0, False)
+        put(3, 1, False)
+
+        y = one("y", [P, PACK, M], F32, tag="late")
         yi = tiles("yi", M // MH, [P, MH, PACK], BF16)
         yq = tiles("yq", M // MH, [P, MH], U32)
         ys = one("ys", [P, M], U8)
-
-        def values_gather(r, on_vector):
-            gather(on_vector, vg[r][:], vt[r][:], l_tok[:])
-
-        def values(r, on_vector):
-            words = vg[r][:].bitcast(F32)
-            bank = ps.tile([P, 2, P], F32, name="bank_v", tag="g2", bufs=4)
-            for u in range(2):
-                nc.tensor.transpose(bank[:, u, :], words[:, u : I // 2 : 2], ident[:])
-            dst = vi[r][:].bitcast(F32).rearrange("p (m u) -> p m u", u=2)
-            src = bank[:].rearrange("p u m -> p m u")
-            if on_vector:
-                nc.vector.tensor_copy(dst, src)
-            else:
-                nc.scalar.copy(dst, src)
-            quantize(vq[r][:], vs[r][:], vi[r][:])
-
-        def product(r, h, on_vector):
-            bank = ps.tile([P, JH], F32, name="bank_o", tag="g2" if on_vector else "acc", bufs=4)
-            nc.tensor.matmul_mx(
-                out=bank[:],
-                lhsT=vq[r][:].bitcast(FP8X4),
-                lhsT_scale=vs[r][:],
-                rhs=gq[h][:].bitcast(FP8X4),
-                rhs_scale=gs[h][:],
-                start=True,
-                stop=True,
-            )
-            if on_vector:
-                piece = y[:, 0, halves[h]]
-            else:
-                piece = sb.tile([P, JH], F32, name="piece", bufs=2, align_bytes=64)[:]
-            if on_vector:
-                nc.vector.tensor_copy(piece, bank[:])
-            else:
-                nc.scalar.copy(piece, bank[:])
-            scatter(on_vector, of[r][:], l_put[:, 16 * h : 16 * h + 16], piece)
 
         def add_old(r, cols, eng):
             eng.tensor_tensor(y[:, r, cols], ot[r][:, cols], of[r][:, cols], ALU.add)
@@ -229,39 +276,15 @@ def tile_attend_tab_larger_put_pl_kernel(
 
         def round_pair(c, q, on_vector):
             cols = slice(c * MH, (c + 1) * MH)
-            dst = yi[c][:, :, 2 * q : 2 * q + 2]
-            src = y[:, 2 * q : 2 * q + 2, cols].rearrange("p r m -> p m r")
-            if on_vector:
-                nc.vector.tensor_copy(dst, src)
-            else:
-                nc.scalar.copy(dst, src)
+            dst = yi[c][:, :, 2 * q : 2 * q + 2].rearrange("p (c i) t -> p c t i", i=4)
+            copy(on_vector, dst, y[:, 2 * q : 2 * q + 2, cols].rearrange("p t (c i) -> p c t i", i=4))
 
         whole = slice(0, M)
-        table(0)
-        table_rows(0)
-        values_gather(0, False)
-        values(0, False)
-        product(0, 0, False)
-        table(1)
-        values_gather(1, False)
-        values(1, False)
-        product(1, 0, False)
-        values_gather(2, True)
-        table_rows(1)
-        values(2, True)
-        product(0, 1, False)
-        product(2, 0, True)
-        product(1, 1, False)
-        product(2, 1, True)
-        values_gather(3, False)
-        values(3, True)
-        product(3, 0, False)
-        product(3, 1, False)
         add_old(0, whole, nc.vector)
         add_old(1, whole, nc.vector)
         add_old(2, whole, nc.vector)
-        round_pair(0, 0, True)
         round_pair(1, 0, True)
+        round_pair(0, 0, False)
         for c in range(M // MH):
             add_old(3, slice(c * MH, (c + 1) * MH), nc.vector)
         round_pair(0, 1, False)

from contextlib import ExitStack

import concourse.mybir as mybir
from concourse.masks import make_identity

D, T, I, J, U, Z, E, M = 512, 2048, 512, 512, 1024, 1024, 512, 1024
FLOPS = 2 * D * I * J * 2 + 2 * I * E * J

F32 = mybir.dt.float32
BF16 = mybir.dt.bfloat16
I32 = mybir.dt.int32
U32 = mybir.dt.uint32
U16 = mybir.dt.uint16
U8 = mybir.dt.uint8
FP8X4 = mybir.dt.float8_e4m3fn_x4
FP4X4 = mybir.dt.float4_e2m1fn_x4
COPY = mybir.ActivationFunctionType.Copy
ALU = mybir.AluOpType

P = 128
PACK = 4
JB = 128
JH = 256
MH = 512


def tile_attend_tab_larger_put_pl_kernel(
    tc, keys_words, keys_scales, notes, users2, rowf, vals, old, offs, offs2, offs3, offs4, out_0, out_1, out_2
):
    nc = tc.nc
    with ExitStack() as ctx:
        sb = ctx.enter_context(tc.tile_pool(name="sb", bufs=1))
        ps = ctx.enter_context(tc.psum_pool(name="ps", bufs=1))

        def one(name, shape, dtype, tag=None):
            return sb.tile(shape, dtype, name=name, tag=tag or name, align_bytes=64)

        def tiles(name, n, shape, dtype):
            return [one("%s%d" % (name, k), shape, dtype) for k in range(n)]

        def bank(name, shape, number):
            return ps.tile(shape, F32, name=name, tag="bank%d" % number)

        l_tok = one("l_tok", [P, I // 16], U16)
        l_note = one("l_note", [P, J // 16], U16)
        l_user = one("l_user", [P, J // 16], U16)
        l_put = one("l_put", [P, J // 16], U16)
        kw = one("kw", [P, T], U16)
        ks = one("ks", [P, T], U8)
        kst = one("kst", [4, 4, T // 4], I32)
        nt = tiles("nt", PACK, [P, U], F32)
        ut = tiles("ut", PACK, [P, Z], F32)
        vt = tiles("vt", PACK, [P, T], F32)
        ot = tiles("ot", PACK, [P, M], F32)
        of = tiles("of", PACK, [P, M], F32)
        rf = one("rf", [P, PACK], F32)
        ident = one("ident", [P, P], F32)

        notes_v = notes.rearrange("(p t) u -> p t u", t=PACK)
        users_v = users2.rearrange("(p t) u -> p t u", t=PACK)
        vals_v = vals.rearrange("(p t) u -> p t u", t=PACK)
        old_v = old.rearrange("(p t) u -> p t u", t=PACK)
        out_v = out_0.rearrange("(p t) u -> p t u", t=PACK)

        nc.sync.dma_start(kst[:], keys_scales[0].bitcast(I32).rearrange("(q c) n -> c q n", c=4))
        nc.sync.dma_start(l_note[:], offs2)
        nc.sync.dma_start(nt[0][:], notes_v[:, 0, :])
        nc.sync.dma_start(l_tok[:], offs)
        nc.sync.dma_start(kw[:].bitcast(I32), keys_words[0].bitcast(I32))
        for t in range(1, PACK):
            nc.sync.dma_start(nt[t][:], notes_v[:, t, :])
        nc.sync.dma_start(l_user[:], offs3)
        for t in range(PACK):
            nc.sync.dma_start(ut[t][:], users_v[:, t, :])
        nc.sync.dma_start(rf[:], rowf.rearrange("(p r) one -> p (r one)", r=PACK))
        nc.sync.dma_start(vt[0][:], vals_v[:, 0, :])
        nc.sync.dma_start(l_put[:], offs4)
        for t in range(1, PACK):
            nc.sync.dma_start(vt[t][:], vals_v[:, t, :])
        for t in range(PACK):
            nc.sync.dma_start(ot[t][:], old_v[:, t, :])

        make_identity(nc, ident[:])
        nc.vector.memset(ks[:].bitcast(I32), 0)
        for r in range(PACK):
            nc.vector.memset(of[r][:], 0.0)

        halves = [slice(h * JH, (h + 1) * JH) for h in range(2)]
        lists = [slice(16 * h, 16 * h + 16) for h in range(2)]

        def gather(on_vector, out, window, offsets):
            if on_vector:
                nc.vector.tensor_copy(out, window.indirect(offsets))
            else:
                nc.scalar.activation(out, window.indirect(offsets), COPY)

        def scatter(on_vector, window, offsets, values):
            if on_vector:
                nc.vector.tensor_copy(window.indirect(offsets), values)
            else:
                nc.scalar.activation(window.indirect(offsets), values, COPY)

        def copy(on_vector, out, in_):
            if on_vector:
                nc.vector.tensor_copy(out, in_)
            else:
                nc.scalar.copy(out, in_)

        def quantize(codes, scales, grouped):
            nc.vector.quantize_mx(out=codes.bitcast(FP8X4), scales=scales, in_=grouped)

        for q in range(4):
            nc.vector.tensor_copy(ks[32 * q : 32 * q + 4, :].bitcast(I32), kst[:, q, :])
        kwg = one("kwg", [P, I], U16)
        nc.vector.tensor_copy(kwg[:], kw[:].indirect(l_tok[:]))
        ksd = one("ksd", [P, I], U8)
        nc.vector.tensor_copy(ksd[:].rearrange("p (r s) -> p s r", r=PACK), ks[:].indirect(l_tok[:]))
        kwd = one("kwd", [P, I], U16)
        nc.vector.tensor_copy(
            kwd[:].rearrange("p (r s) -> p r s", r=PACK), kwg[:].rearrange("p (s r) -> p r s", r=PACK)
        )

        def gather_planes(dst, planes, offsets, engines):
            for t in range(PACK - 1):
                gather(engines[t], dst[:, t, :], planes[t][:], offsets[:])
            for h in range(2):
                gather(h == 0, dst[:, PACK - 1, halves[h]], planes[PACK - 1][:], offsets[:, lists[h]])

        def weave_quant(src, woven, codes, scales):
            for h in range(2):
                nc.vector.tensor_copy(
                    woven[h][:].rearrange("p (c i) t -> p c t i", i=4),
                    src[:, :, halves[h]].rearrange("p t (c i) -> p c t i", i=4),
                )
            for h in range(2):
                quantize(codes[h][:], scales[h][:], woven[h][:].rearrange("p j t -> p (j t)"))

        def scores(acc, codes, scales):
            for r in range(PACK):
                cols = slice(r * P, (r + 1) * P)
                nc.tensor.matmul_mx(
                    out=acc[:, r, :],
                    lhsT=kwd[:, cols].bitcast(FP4X4),
                    lhsT_scale=ksd[:, cols],
                    rhs=codes.bitcast(FP8X4),
                    rhs_scale=scales,
                    start=True,
                    stop=True,
                )

        ng = one("ng", [P, PACK, J], BF16)
        gather_planes(ng, nt, l_note, [False, False, False])
        ni = tiles("ni", 2, [P, JH, PACK], BF16)
        nq = tiles("nq", 2, [P, JH], U32)
        ns = tiles("ns", 2, [P, JH], U8)
        weave_quant(ng, ni, nq, ns)

        ug = one("ug", [P, PACK, J], BF16)
        gather_planes(ug, ut, l_user, [False, False, True])

        g1 = []
        for h in range(2):
            g1.append(one("g1_%d" % h, [P, JH, PACK], F32, tag="ut%d" % (2 * h + 1)))
            for k in range(2):
                cols = slice(k * JB, (k + 1) * JB)
                acc = bank("acc_g1", [P, PACK, JB], 2 * h + k)
                scores(acc, nq[h][:, cols], ns[h][:, cols])
                nc.scalar.copy(g1[h][:, cols, :], acc[:].rearrange("p r n -> p n r"))

        ui = tiles("ui", 2, [P, JH, PACK], BF16)
        uq = tiles("uq", 2, [P, JH], U32)
        us = tiles("us", 2, [P, JH], U8)
        weave_quant(ug, ui, uq, us)

        g0 = tiles("g0", 2, [P, JH, PACK], F32)
        gq = {}
        gs = tiles("gs", 2, [P, JH], U8)

        def larger(h, k):
            cols = slice(k * JB, (k + 1) * JB)
            acc = bank("acc_g2", [P, PACK, JB], 4 + 2 * h + k)
            scores(acc, uq[h][:, cols], us[h][:, cols])
            nc.vector.tensor_tensor(g0[h][:, cols, :], acc[:].rearrange("p r n -> p n r"), g1[h][:, cols, :], ALU.max)

        gr = {}

        def scale_rows(h, tag):
            gr[h] = one("gr%d" % h, [P, JH, PACK], BF16, tag=tag)
            nc.vector.tensor_tensor(gr[h][:], g0[h][:], rf[:].unsqueeze(1).to_broadcast([P, JH, PACK]), ALU.mult)

        def quant_table(h, tag):
            gq[h] = one("gq%d" % h, [P, JH], U32, tag=tag)
            quantize(gq[h][:], gs[h][:], gr[h][:].rearrange("p j t -> p (j t)"))

        vg = tiles("vg", PACK, [P, I], BF16)
        vq = tiles("vq", PACK, [P, P], U32)
        vs = tiles("vs", PACK, [P, P], U8)

        woven_values = {}

        def turn_values(r, on_vector, number, tag):
            words = vg[r][:].bitcast(F32)
            acc = bank("acc_v", [P, 2, P], number)
            for u in range(2):
                nc.tensor.transpose(acc[:, u, :], words[:, u : I // 2 : 2], ident[:])
            vi = one("vi%d" % r, [P, P * PACK], BF16, tag=tag)
            copy(on_vector, vi[:].bitcast(F32).rearrange("p (m u) -> p m u", u=2), acc[:].rearrange("p u m -> p m u"))
            woven_values[r] = vi

        def quant_values(r):
            quantize(vq[r][:], vs[r][:], woven_values[r][:])

        pieces = {}

        def products(name, units, on_vector, number, tag):
            acc = bank("acc_o", [P, J], number)
            for k, (r, h) in enumerate(units):
                nc.tensor.matmul_mx(
                    out=acc[:, halves[k]],
                    lhsT=vq[r][:].bitcast(FP8X4),
                    lhsT_scale=vs[r][:],
                    rhs=gq[h][:].bitcast(FP8X4),
                    rhs_scale=gs[h][:],
                    start=True,
                    stop=True,
                )
            staged = one(name, [P, J], F32, tag=tag)
            copy(on_vector, staged[:], acc[:])
            for k, unit in enumerate(units):
                pieces[unit] = staged[:, halves[k]]

        def put(r, h, on_vector):
            scatter(on_vector, of[r][:], l_put[:, lists[h]], pieces[r, h])

        larger(0, 0)
        larger(0, 1)
        larger(1, 0)
        scale_rows(0, None)
        gather(False, vg[0][:], vt[0][:], l_tok[:])
        gather(False, vg[1][:], vt[1][:], l_tok[:])
        turn_values(0, False, 0, "vt1")
        turn_values(1, False, 1, None)
        quant_values(0)
        quant_table(0, None)
        quant_values(1)
        larger(1, 1)
        gather(False, vg[2][:], vt[2][:], l_tok[:])
        products("first", ((0, 0), (1, 0)), False, 1, "vt2")
        turn_values(2, True, 4, None)
        scale_rows(1, "vi1")
        gather(True, vg[3][:], vt[3][:], l_tok[:])
        quant_table(1, "vt3")
        quant_values(2)
        put(0, 0, False)
        put(1, 0, False)
        products("second", ((0, 1), (1, 1)), False, 4, "vt2")
        turn_values(3, True, 5, None)
        quant_values(3)
        products("own", ((2, 0), (2, 1)), True, 6, "late")
        put(2, 0, True)
        put(2, 1, True)
        put(0, 1, False)
        put(1, 1, False)
        products("third", ((3, 0), (3, 1)), False, 0, None)
        put(3, 0, False)
        put(3, 1, False)

        y = one("y", [P, PACK, M], F32, tag="late")
        yi = tiles("yi", M // MH, [P, MH, PACK], BF16)
        yq = tiles("yq", M // MH, [P, MH], U32)
        ys = one("ys", [P, M], U8)

        def add_old(r, cols, eng):
            eng.tensor_tensor(y[:, r, cols], ot[r][:, cols], of[r][:, cols], ALU.add)
            nc.sync.dma_start(out_v[:, r, cols], y[:, r, cols])

        def round_pair(c, q, on_vector):
            cols = slice(c * MH, (c + 1) * MH)
            dst = yi[c][:, :, 2 * q : 2 * q + 2].rearrange("p (c i) t -> p c t i", i=4)
            copy(on_vector, dst, y[:, 2 * q : 2 * q + 2, cols].rearrange("p t (c i) -> p c t i", i=4))

        whole = slice(0, M)
        add_old(0, whole, nc.vector)
        add_old(1, whole, nc.vector)
        add_old(2, whole, nc.vector)
        round_pair(1, 0, True)
        round_pair(0, 0, False)
        for c in range(M // MH):
            add_old(3, slice(c * MH, (c + 1) * MH), nc.vector)
        round_pair(0, 1, False)
        round_pair(1, 1, True)
        words_out = out_1[0].rearrange("p m t -> p (m t)").bitcast(I32)
        for c in (1, 0):
            cols = slice(c * MH, (c + 1) * MH)
            quantize(yq[c][:], ys[:, cols], yi[c][:].rearrange("p m t -> p (m t)"))
            nc.sync.dma_start(words_out[:, cols], yq[c][:].bitcast(I32))
        for q in range(4):
            eng = nc.sync if q % 2 == 0 else nc.scalar
            eng.dma_start(out_2[0, 4 * q : 4 * q + 4, :].bitcast(I32), ys[32 * q : 32 * q + 4, :].bitcast(I32))
